import numpy as np
import ml_dtypes


def mxq(x, axis, fmt="e4m3"):
    dtype, down = {"e4m3": (ml_dtypes.float8_e4m3fn, 7), "e5m2": (ml_dtypes.float8_e5m2, 14)}[fmt]
    v = np.moveaxis(np.asarray(x, np.float32).astype(ml_dtypes.bfloat16).astype(np.float64), axis, -1)
    blocks = v.reshape(v.shape[:-1] + (-1, 32))
    amax = np.abs(blocks).max(-1, keepdims=True)
    byte = np.maximum(np.where(amax > 0, np.frexp(amax)[1] - 1 + 127, 0) - down, 1)
    scale = np.exp2(byte - 127.0)
    codes = (blocks / scale).astype(np.float32).astype(dtype).astype(np.float64)
    return np.moveaxis((codes * scale).reshape(v.shape), -1, axis)


WIDE = False


def mx_kscale(k):
    if not WIDE:
        return np.ones(k)
    levels = np.array([10, -10, 5, -5, 0])
    if k % 512:
        return np.exp2(np.random.permutation(np.resize(levels, k // 32))).repeat(32)
    a = np.empty((k // 512, 16))
    for p in range(k // 512):
        a[p, :8] = np.random.permutation(np.resize(levels, 8))
        for g in range(8):
            far = levels[np.abs(levels - a[p, g]) >= 10]
            a[p, g + 8] = far[np.random.randint(len(far))]
    return np.exp2(a.ravel()).repeat(32)


def f64(x):
    return np.asarray(x).astype(np.float64)


def striped(idx):
    return np.tile(idx.reshape(-1, 16).T, (8, 1)).astype(np.uint16)


def unstriped(offs):
    return offs[:16].T.reshape(-1).astype(np.int64)


def pack_weight(w):
    k, n = w.shape
    w = f64(np.asarray(w, np.float32).astype(ml_dtypes.bfloat16)).reshape(k // 32, 32, n)
    amax = np.abs(w).max(1)
    byte = np.clip(np.where(amax > 0, np.frexp(amax)[1] - 1 + 127 - 7, 1), 1, 254)
    scaled = (w * np.exp2(127.0 - byte)[:, None, :]).reshape(k, n).astype(np.float32)
    words = np.ascontiguousarray(scaled.reshape(k // 512, 128, 4, n).transpose(0, 1, 3, 2)).astype(ml_dtypes.float8_e4m3fn).view(np.uint8)
    return words, np.ascontiguousarray(byte.astype(np.uint8).reshape(k // 512, 16, n))


def unpack_weight(words, scales):
    g, p, n, _ = words.shape
    vals = np.ascontiguousarray(words).view(ml_dtypes.float8_e4m3fn).astype(np.float64) * np.repeat(np.exp2(scales.astype(np.float64) - 127.0), 8, axis=1)[..., None]
    return vals.transpose(0, 1, 3, 2).reshape(g * 512, n)


K, T, S, H, N, V = 512, 1024, 512, 512, 256, 256
P = 2 ** 7


def setup_inputs():
    n = np.random.standard_normal
    s = mx_kscale(K)[:, None]
    u = mx_kscale(H)
    packed_xT = pack_weight(n((K, T)) * s)
    return {
        "x_words": packed_xT[0],
        "x_scales": packed_xT[1],
        "w1": (n((K, H)) / np.sqrt(K) / s).astype(np.float32),
        "m1": (np.tile(n(S) * 0.7, (P, 1))).astype(np.float32),
        "m2": (np.tile(n(V) * 0.7, (P, 1))).astype(np.float32),
        "unit": (np.random.uniform(0.5, 1.0, (H, 1)) * u[:, None]).astype(np.float32),
        "t1": (n((H, N)) / np.sqrt(2 * H) / u[:, None]).astype(np.float32),
        "offs": striped(np.random.permutation(T)[:S]),
        "fa": striped(np.random.randint(0, S, S)),
        "fb": striped(np.random.randint(0, S, S)),
        "fc": striped(np.random.randint(0, V, V)),
        "fd": striped(np.random.randint(0, S, V)),
    }


def reference(x_words, x_scales, w1, m1, m2, unit, t1, offs, fa, fb, fc, fd):
    xq = unpack_weight(x_words, x_scales)[:, unstriped(offs)]
    y = mxq(f64(w1), 0, "e4m3").T @ xq
    p1 = (y[:, unstriped(fa)] * y[:, unstriped(fb)]) * f64(m1)[:1]
    x1 = p1.reshape(len(p1), -1, 2).sum(axis=2)
    x2 = (x1[:, unstriped(fc)] * y[:, unstriped(fd)]) * f64(m2)[:1]
    z0 = f64(unit) * x2
    return mxq(f64(t1), 0, "e4m3").T @ mxq(z0, 0, "e4m3")

@@ -1,0 +1,228 @@
+from contextlib import ExitStack
+
+import concourse.mybir as mybir
+from concourse.masks import make_identity
+
+K, T, S, H, N, V = 512, 1024, 512, 512, 256, 256
+FLOPS = 2 * K * H * S + 2 * H * N * V
+
+F32 = mybir.dt.float32
+BF16 = mybir.dt.bfloat16
+I32 = mybir.dt.int32
+U32 = mybir.dt.uint32
+U16 = mybir.dt.uint16
+U8 = mybir.dt.uint8
+FP8X4 = mybir.dt.float8_e4m3fn_x4
+MULT = mybir.AluOpType.mult
+COPY = mybir.ActivationFunctionType.Copy
+
+P = 128
+PACK = 4
+SPARE = 8
+
+
+def tile_picked_ycin_deep_p_kernel(
+    tc, x_words, x_scales, w1, m1, m2, unit, t1, offs, fa, fb, fc, fd, out
+):
+    nc = tc.nc
+    with ExitStack() as ctx:
+        lists = ctx.enter_context(tc.tile_pool(name="lists", bufs=1))
+        sb = ctx.enter_context(tc.tile_pool(name="sb", bufs=1))
+        psum = ctx.enter_context(tc.psum_pool(name="psum", bufs=1))
+
+        offs_sb = lists.tile([P, S // 16], U16, name="offs_sb")
+        fa_sb = lists.tile([P, S // 16], U16, name="fa_sb")
+        fb_sb = lists.tile([P, S // 16], U16, name="fb_sb")
+        fc_sb = lists.tile([P, V // 16], U16, name="fc_sb")
+        fd_sb = lists.tile([P, V // 16], U16, name="fd_sb")
+
+        xs_all = sb.tile([P, T], U8, name="xs_all", align_bytes=64)
+        xw_all = sb.tile([P, T], U32, name="xw_all", align_bytes=64)
+        for q in range(4):
+            rows = x_scales[0, 4 * q : 4 * q + 4, :].bitcast(I32)
+            nc.sync.dma_start(
+                out=xs_all[32 * q : 32 * q + 32, :].bitcast(I32),
+                in_=rows.unsqueeze(0).to_broadcast([8, 4, T // 4]),
+            )
+        nc.sync.dma_start(out=offs_sb[:], in_=offs)
+        nc.sync.dma_start(
+            out=xw_all[:].bitcast(I32),
+            in_=x_words[0].rearrange("p n t -> p (n t)").bitcast(I32),
+        )
+        w1_rows = w1.rearrange("(p j) c -> p j c", j=PACK)
+        w_raw = []
+        for h in range(2):
+            w_half = sb.tile([P, PACK, H // 2], F32, name="w_raw%d" % h)
+            nc.sync.dma_start(out=w_half[:], in_=w1_rows[:, :, h * (H // 2) : (h + 1) * (H // 2)])
+            w_raw.append(w_half)
+        m1_sb = sb.tile([P, S], F32, name="m1_sb")
+        m2_sb = sb.tile([P, V], F32, name="m2_sb")
+        unit_sb = sb.tile([P, PACK], F32, name="unit_sb")
+        t_raw = sb.tile([P, PACK, N], F32, name="t_raw")
+        nc.sync.dma_start(out=fa_sb[:], in_=fa)
+        nc.sync.dma_start(out=m1_sb[:], in_=m1)
+        nc.sync.dma_start(out=fb_sb[:], in_=fb)
+        nc.sync.dma_start(out=t_raw[:], in_=t1.rearrange("(p j) n -> p j n", j=PACK))
+        nc.sync.dma_start(out=m2_sb[:], in_=m2)
+        nc.sync.dma_start(out=unit_sb[:], in_=unit.rearrange("(p t) o -> p (t o)", t=PACK))
+        nc.sync.dma_start(out=fd_sb[:], in_=fd)
+        nc.sync.dma_start(out=fc_sb[:], in_=fc)
+
+        y = [sb.tile([P, S + SPARE], F32, name="y%d" % t) for t in range(PACK)]
+        x1 = [sb.tile([P, V + SPARE], F32, name="x1_%d" % t) for t in range(PACK)]
+        for t in range(PACK):
+            nc.gpsimd.memset(y[t][:, S:], 0.0)
+        for t in range(PACK):
+            nc.gpsimd.memset(x1[t][:, V:], 0.0)
+
+        ident = sb.tile([P, P], F32, name="ident")
+        make_identity(nc, ident[:])
+
+        xs = sb.tile([P, S], U8, name="xs", align_bytes=64)
+        xw = sb.tile([P, S], U32, name="xw", align_bytes=64)
+        nc.vector.tensor_copy(out=xs[:], in_=xs_all[:].indirect(offs_sb[:]))
+        nc.vector.tensor_copy(out=xw[:], in_=xw_all[:].indirect(offs_sb[:]))
+
+        w_bf = [sb.tile([P, 2, P, PACK], BF16, name="w_bf%d" % u, align_bytes=64) for u in range(2)]
+        for h in range(2):
+            src = w_raw[h][:].rearrange("p j (m t) -> p m j t", t=PACK)
+            for u in range(2):
+                dst = w_bf[u][:, :, h * (P // 2) : (h + 1) * (P // 2), :].rearrange("p t m j -> p m j t")
+                if u == 0:
+                    nc.vector.tensor_copy(out=dst, in_=src[:, :, :, 0:2])
+                else:
+                    nc.scalar.copy(out=dst, in_=src[:, :, :, 2:4])
+
+        w_codes = [sb.tile([P, P], U32, name="w_codes%d" % t, align_bytes=64) for t in range(PACK)]
+        w_scales = [sb.tile([P, P], U8, name="w_scales%d" % t, align_bytes=64) for t in range(PACK)]
+        for t in range(PACK):
+            nc.vector.quantize_mx(
+                out=w_codes[t][:].bitcast(FP8X4),
+                scales=w_scales[t][:],
+                in_=w_bf[t // 2][:, t % 2].rearrange("p m j -> p (m j)"),
+            )
+            y_ps = psum.tile([P, S], F32, name="mx_ps", bufs=4)
+            nc.tensor.matmul_mx(
+                out=y_ps[:],
+                lhsT=w_codes[t][:].bitcast(FP8X4),
+                lhsT_scale=w_scales[t][:],
+                rhs=xw[:].bitcast(FP8X4),
+                rhs_scale=xs[:],
+                start=True,
+                stop=True,
+            )
+            nc.scalar.copy(out=y[t][:, :S], in_=y_ps[:])
+
+        t_bf = sb.tile([P, N, PACK], BF16, name="t_bf", align_bytes=64)
+        nc.scalar.copy(
+            out=t_bf[:].rearrange("p (c i) j -> p c j i", i=4),
+            in_=t_raw[:].rearrange("p j (c i) -> p c j i", i=4),
+        )
+        um = [sb.tile([P, V], F32, name="um%d" % t) for t in range(PACK)]
+        for t in range(PACK):
+            nc.scalar.activation(out=um[t][:], in_=m2_sb[:], func=COPY, scale=unit_sb[:, t : t + 1])
+
+        ga = [sb.tile([P, S], F32, name="ga%d" % t) for t in range(PACK)]
+        p1 = [sb.tile([P, S], F32, name="p1_%d" % t) for t in range(PACK)]
+        gd = [sb.tile([P, V], F32, name="gd%d" % t) for t in range(PACK)]
+        z0 = [sb.tile([P, PACK, P], F32, name="z0_%d" % h) for h in range(2)]
+
+        def take_a(t):
+            nc.vector.tensor_tensor(ga[t][:], y[t][:].indirect(fa_sb[:]), m1_sb[:], MULT)
+
+        def take_b(t):
+            nc.vector.tensor_tensor(p1[t][:], y[t][:].indirect(fb_sb[:]), ga[t][:], MULT)
+
+        def pair(t):
+            pv = p1[t][:].rearrange("p (h v d) -> p h d v", h=2, d=2)
+            turned_ps = psum.tile([P, 2, P], F32, name="turned_ps", bufs=2)
+            for h in range(2):
+                for d in range(2):
+                    nc.tensor.matmul(
+                        turned_ps[:, h, :], lhsT=pv[:, h, d, :], rhs=ident[:],
+                        start=(d == 0), stop=(d == 1), is_transpose=True,
+                    )
+            turned = sb.tile([P, 2, P], F32, name="turned", bufs=2)
+            nc.scalar.copy(out=turned[:], in_=turned_ps[:])
+            back_ps = psum.tile([P, 2, P], F32, name="back_ps", bufs=2)
+            for h in range(2):
+                nc.tensor.transpose(back_ps[:, h, :], turned[:, h, :], ident[:])
+            nc.scalar.copy(out=x1[t][:, :V], in_=back_ps[:].rearrange("p h v -> p (h v)"))
+
+        def take_d(t):
+            nc.vector.tensor_tensor(gd[t][:], y[t][:].indirect(fd_sb[:]), um[t][:], MULT)
+
+        def take_c(t, h):
+            nc.vector.tensor_tensor(
+                z0[h][:, t, :], x1[t][:].indirect(fc_sb[:, 8 * h : 8 * h + 8]), gd[t][:, h * P : (h + 1) * P], MULT
+            )
+
+        t_codes = sb.tile([P, N], U32, name="t_codes", align_bytes=64)
+        t_scales = sb.tile([P, N], U8, name="t_scales", align_bytes=64)
+
+        for t in (0, 2):
+            take_a(t)
+            take_a(t + 1)
+            take_b(t)
+            pair(t)
+            take_b(t + 1)
+            pair(t + 1)
+        nc.vector.quantize_mx(
+            out=t_codes[:].bitcast(FP8X4), scales=t_scales[:], in_=t_bf[:].rearrange("p n j -> p (n j)")
+        )
+        for t in range(PACK):
+            take_d(t)
+
+        z_bf = [sb.tile([P, P, PACK], BF16, name="z_bf%d" % h, align_bytes=64) for h in range(2)]
+        z_codes = [sb.tile([P, P], U32, name="z_codes%d" % h, align_bytes=64) for h in range(2)]
+        z_scales = [sb.tile([P, P], U8, name="z_scales%d" % h, align_bytes=64) for h in range(2)]
+
+        def weave(h, copy):
+            copy(
+                out=z_bf[h][:].rearrange("p (c i) t -> p c t i", i=4),
+                in_=z0[h][:].rearrange("p t (c i) -> p c t i", i=4),
+            )
+
+        def quantize_z(h):
+            nc.vector.quantize_mx(
+                out=z_codes[h][:].bitcast(FP8X4),
+                scales=z_scales[h][:],
+                in_=z_bf[h][:].rearrange("p v t -> p (v t)"),
+            )
+
+        def product(h, b, dst):
+            nc.tensor.matmul_mx(
+                out=dst,
+                lhsT=t_codes[:, b * P : (b + 1) * P].bitcast(FP8X4),
+                lhsT_scale=t_scales[:, b * P : (b + 1) * P],
+                rhs=z_codes[h][:].bitcast(FP8X4),
+                rhs_scale=z_scales[h][:],
+                start=True,
+                stop=True,
+            )
+
+        for t in range(PACK):
+            take_c(t, 0)
+        weave(0, nc.scalar.copy)
+        for t in range(PACK):
+            take_c(t, 1)
+        quantize_z(0)
+        o_ps = psum.tile([P, 2, P], F32, name="mx_ps", bufs=4)
+        for b in range(2):
+            product(0, b, o_ps[:, b, :])
+        o_first = sb.tile([P, 2, P], F32, name="o_first")
+        nc.scalar.copy(out=o_first[:], in_=o_ps[:])
+        nc.sync.dma_start(out=out[:, :P].rearrange("(b p) v -> p b v", p=P), in_=o_first[:])
+
+        weave(1, nc.vector.tensor_copy)
+        quantize_z(1)
+        for b in range(2):
+            o_ps = psum.tile([P, P], F32, name="mx_ps", bufs=4)
+            product(1, b, o_ps[:])
+            o_sb = sb.tile([P, P], F32, name="o_sb%d" % b)
+            if b == 0:
+                nc.vector.tensor_copy(out=o_sb[:], in_=o_ps[:])
+                nc.sync.dma_start(out=out[b * P : (b + 1) * P, P:], in_=o_sb[:])
+            else:
+                nc.scalar.copy(out=o_sb[:], in_=o_ps[:])
+                nc.scalar.dma_start(out=out[b * P : (b + 1) * P, P:], in_=o_sb[:])

@@ -38,17 +38,17 @@ def tile_picked_ycin_deep_p_kernel(
 
         xs_all = sb.tile([P, T], U8, name="xs_all", align_bytes=64)
         xw_all = sb.tile([P, T], U32, name="xw_all", align_bytes=64)
-        for q in range(4):
-            rows = x_scales[0, 4 * q : 4 * q + 4, :].bitcast(I32)
-            nc.sync.dma_start(
-                out=xs_all[32 * q : 32 * q + 32, :].bitcast(I32),
-                in_=rows.unsqueeze(0).to_broadcast([8, 4, T // 4]),
-            )
-        nc.sync.dma_start(out=offs_sb[:], in_=offs)
+        nc.gpsimd.memset(xs_all[:].bitcast(I32), 0)
         nc.sync.dma_start(
             out=xw_all[:].bitcast(I32),
             in_=x_words[0].rearrange("p n t -> p (n t)").bitcast(I32),
         )
+        nc.sync.dma_start(out=offs_sb[:], in_=offs)
+        for q in range(4):
+            nc.sync.dma_start(
+                out=xs_all[32 * q : 32 * q + 4, :].bitcast(I32),
+                in_=x_scales[0, 4 * q : 4 * q + 4, :].bitcast(I32),
+            )
         w1_rows = w1.rearrange("(p j) c -> p j c", j=PACK)
         w_raw = []
         for h in range(2):
@@ -80,38 +80,48 @@ def tile_picked_ycin_deep_p_kernel(
 
         xs = sb.tile([P, S], U8, name="xs", align_bytes=64)
         xw = sb.tile([P, S], U32, name="xw", align_bytes=64)
-        nc.vector.tensor_copy(out=xs[:], in_=xs_all[:].indirect(offs_sb[:]))
         nc.vector.tensor_copy(out=xw[:], in_=xw_all[:].indirect(offs_sb[:]))
+        nc.vector.tensor_copy(out=xs[:], in_=xs_all[:].indirect(offs_sb[:]))
 
         w_bf = [sb.tile([P, 2, P, PACK], BF16, name="w_bf%d" % u, align_bytes=64) for u in range(2)]
+        w_codes = [sb.tile([P, 2, P], U32, name="w_codes%d" % u, align_bytes=64) for u in range(2)]
+        w_scales = [sb.tile([P, 2, P], U8, name="w_scales%d" % u, align_bytes=64) for u in range(2)]
         for h in range(2):
             src = w_raw[h][:].rearrange("p j (m t) -> p m j t", t=PACK)
-            for u in range(2):
-                dst = w_bf[u][:, :, h * (P // 2) : (h + 1) * (P // 2), :].rearrange("p t m j -> p m j t")
-                if u == 0:
-                    nc.vector.tensor_copy(out=dst, in_=src[:, :, :, 0:2])
-                else:
-                    nc.scalar.copy(out=dst, in_=src[:, :, :, 2:4])
+            cols = slice(h * (P // 2), (h + 1) * (P // 2))
+            first_copy = nc.scalar.copy if h == 0 else nc.vector.tensor_copy
+            first_copy(out=w_bf[0][:, :, cols, :].rearrange("p t m j -> p m j t"), in_=src[:, :, :, 0:2])
+            nc.scalar.copy(out=w_bf[1][:, :, cols, :].rearrange("p t m j -> p m j t"), in_=src[:, :, :, 2:4])
+            for t in range(2):
+                nc.vector.quantize_mx(
+                    out=w_codes[0][:, t, cols].bitcast(FP8X4),
+                    scales=w_scales[0][:, t, cols],
+                    in_=w_bf[0][:, t, cols, :].rearrange("p m j -> p (m j)"),
+                )
 
-        w_codes = [sb.tile([P, P], U32, name="w_codes%d" % t, align_bytes=64) for t in range(PACK)]
-        w_scales = [sb.tile([P, P], U8, name="w_scales%d" % t, align_bytes=64) for t in range(PACK)]
-        for t in range(PACK):
-            nc.vector.quantize_mx(
-                out=w_codes[t][:].bitcast(FP8X4),
-                scales=w_scales[t][:],
-                in_=w_bf[t // 2][:, t % 2].rearrange("p m j -> p (m j)"),
-            )
-            y_ps = psum.tile([P, S], F32, name="mx_ps", bufs=4)
+        def project(t, cols, copy):
+            y_ps = psum.tile([P, cols.stop - cols.start], F32, name="mx_ps", bufs=4)
             nc.tensor.matmul_mx(
                 out=y_ps[:],
-                lhsT=w_codes[t][:].bitcast(FP8X4),
-                lhsT_scale=w_scales[t][:],
-                rhs=xw[:].bitcast(FP8X4),
-                rhs_scale=xs[:],
+                lhsT=w_codes[t // 2][:, t % 2, :].bitcast(FP8X4),
+                lhsT_scale=w_scales[t // 2][:, t % 2, :],
+                rhs=xw[:, cols].bitcast(FP8X4),
+                rhs_scale=xs[:, cols],
                 start=True,
                 stop=True,
             )
-            nc.scalar.copy(out=y[t][:, :S], in_=y_ps[:])
+            copy(out=y[t][:, cols], in_=y_ps[:])
+
+        project(0, slice(0, S // 2), nc.scalar.copy)
+        project(0, slice(S // 2, S), nc.vector.tensor_copy)
+        project(1, slice(0, S), nc.scalar.copy)
+        nc.vector.quantize_mx(
+            out=w_codes[1][:].rearrange("p t m -> p (t m)").bitcast(FP8X4),
+            scales=w_scales[1][:].rearrange("p t m -> p (t m)"),
+            in_=w_bf[1][:].rearrange("p t m j -> p (t m j)"),
+        )
+        project(2, slice(0, S), nc.scalar.copy)
+        project(3, slice(0, S), nc.scalar.copy)
 
         t_bf = sb.tile([P, N, PACK], BF16, name="t_bf", align_bytes=64)
         nc.scalar.copy(

@@ -59,21 +59,19 @@ def tile_picked_ycin_deep_p_kernel(
         m2_sb = sb.tile([P, V], F32, name="m2_sb")
         unit_sb = sb.tile([P, PACK], F32, name="unit_sb")
         t_raw = sb.tile([P, PACK, N], F32, name="t_raw")
+        nc.sync.dma_start(out=t_raw[:], in_=t1.rearrange("(p j) n -> p j n", j=PACK))
         nc.sync.dma_start(out=fa_sb[:], in_=fa)
         nc.sync.dma_start(out=m1_sb[:], in_=m1)
         nc.sync.dma_start(out=fb_sb[:], in_=fb)
-        nc.sync.dma_start(out=t_raw[:], in_=t1.rearrange("(p j) n -> p j n", j=PACK))
         nc.sync.dma_start(out=m2_sb[:], in_=m2)
         nc.sync.dma_start(out=unit_sb[:], in_=unit.rearrange("(p t) o -> p (t o)", t=PACK))
         nc.sync.dma_start(out=fd_sb[:], in_=fd)
         nc.sync.dma_start(out=fc_sb[:], in_=fc)
 
         y = [sb.tile([P, S + SPARE], F32, name="y%d" % t) for t in range(PACK)]
-        x1 = [sb.tile([P, V + SPARE], F32, name="x1_%d" % t) for t in range(PACK)]
+        x1 = [sb.tile([P, V], F32, name="x1_%d" % t) for t in range(PACK)]
         for t in range(PACK):
-            nc.gpsimd.memset(y[t][:, S:], 0.0)
-        for t in range(PACK):
-            nc.gpsimd.memset(x1[t][:, V:], 0.0)
+            nc.vector.memset(y[t][:, S:], 0.0)
 
         ident = sb.tile([P, P], F32, name="ident")
         make_identity(nc, ident[:])
@@ -113,7 +111,7 @@ def tile_picked_ycin_deep_p_kernel(
             copy(out=y[t][:, cols], in_=y_ps[:])
 
         project(0, slice(0, S // 2), nc.scalar.copy)
-        project(0, slice(S // 2, S), nc.vector.tensor_copy)
+        project(0, slice(S // 2, S), nc.scalar.copy)
         project(1, slice(0, S), nc.scalar.copy)
         nc.vector.quantize_mx(
             out=w_codes[1][:].rearrange("p t m -> p (t m)").bitcast(FP8X4),
@@ -124,9 +122,14 @@ def tile_picked_ycin_deep_p_kernel(
         project(3, slice(0, S), nc.scalar.copy)
 
         t_bf = sb.tile([P, N, PACK], BF16, name="t_bf", align_bytes=64)
-        nc.scalar.copy(
+        nc.vector.tensor_copy(
             out=t_bf[:].rearrange("p (c i) j -> p c j i", i=4),
             in_=t_raw[:].rearrange("p j (c i) -> p c j i", i=4),
+        )
+        t_codes = sb.tile([P, N], U32, name="t_codes", align_bytes=64)
+        t_scales = sb.tile([P, N], U8, name="t_scales", align_bytes=64)
+        nc.vector.quantize_mx(
+            out=t_codes[:].bitcast(FP8X4), scales=t_scales[:], in_=t_bf[:].rearrange("p n j -> p (n j)")
         )
         um = [sb.tile([P, V], F32, name="um%d" % t) for t in range(PACK)]
         for t in range(PACK):
@@ -157,7 +160,7 @@ def tile_picked_ycin_deep_p_kernel(
             back_ps = psum.tile([P, 2, P], F32, name="back_ps", bufs=2)
             for h in range(2):
                 nc.tensor.transpose(back_ps[:, h, :], turned[:, h, :], ident[:])
-            nc.scalar.copy(out=x1[t][:, :V], in_=back_ps[:].rearrange("p h v -> p (h v)"))
+            nc.scalar.copy(out=x1[t][:], in_=back_ps[:].rearrange("p h v -> p (h v)"))
 
         def take_d(t):
             nc.vector.tensor_tensor(gd[t][:], y[t][:].indirect(fd_sb[:]), um[t][:], MULT)
@@ -167,9 +170,6 @@ def tile_picked_ycin_deep_p_kernel(
                 z0[h][:, t, :], x1[t][:].indirect(fc_sb[:, 8 * h : 8 * h + 8]), gd[t][:, h * P : (h + 1) * P], MULT
             )
 
-        t_codes = sb.tile([P, N], U32, name="t_codes", align_bytes=64)
-        t_scales = sb.tile([P, N], U8, name="t_scales", align_bytes=64)
-
         for t in (0, 2):
             take_a(t)
             take_a(t + 1)
@@ -177,9 +177,6 @@ def tile_picked_ycin_deep_p_kernel(
             pair(t)
             take_b(t + 1)
             pair(t + 1)
-        nc.vector.quantize_mx(
-            out=t_codes[:].bitcast(FP8X4), scales=t_scales[:], in_=t_bf[:].rearrange("p n j -> p (n j)")
-        )
         for t in range(PACK):
             take_d(t)
 

@@ -44,17 +44,15 @@ def tile_picked_ycin_deep_p_kernel(
             in_=x_words[0].rearrange("p n t -> p (n t)").bitcast(I32),
         )
         nc.sync.dma_start(out=offs_sb[:], in_=offs)
+        w1_rows = w1.rearrange("(p j) c -> p j c", j=PACK)
+        w_raw = [sb.tile([P, PACK, H // 2], F32, name="w_raw%d" % h) for h in range(2)]
+        nc.sync.dma_start(out=w_raw[0][:], in_=w1_rows[:, :, : H // 2])
         for q in range(4):
             nc.sync.dma_start(
                 out=xs_all[32 * q : 32 * q + 4, :].bitcast(I32),
                 in_=x_scales[0, 4 * q : 4 * q + 4, :].bitcast(I32),
             )
-        w1_rows = w1.rearrange("(p j) c -> p j c", j=PACK)
-        w_raw = []
-        for h in range(2):
-            w_half = sb.tile([P, PACK, H // 2], F32, name="w_raw%d" % h)
-            nc.sync.dma_start(out=w_half[:], in_=w1_rows[:, :, h * (H // 2) : (h + 1) * (H // 2)])
-            w_raw.append(w_half)
+        nc.sync.dma_start(out=w_raw[1][:], in_=w1_rows[:, :, H // 2 :])
         m1_sb = sb.tile([P, S], F32, name="m1_sb")
         m2_sb = sb.tile([P, V], F32, name="m2_sb")
         unit_sb = sb.tile([P, PACK], F32, name="unit_sb")
@@ -87,8 +85,12 @@ def tile_picked_ycin_deep_p_kernel(
         for h in range(2):
             src = w_raw[h][:].rearrange("p j (m t) -> p m j t", t=PACK)
             cols = slice(h * (P // 2), (h + 1) * (P // 2))
-            first_copy = nc.scalar.copy if h == 0 else nc.vector.tensor_copy
-            first_copy(out=w_bf[0][:, :, cols, :].rearrange("p t m j -> p m j t"), in_=src[:, :, :, 0:2])
+            dst = w_bf[0][:, :, cols, :].rearrange("p t m j -> p m j t")
+            if h == 0:
+                nc.scalar.copy(out=dst, in_=src[:, :, :, 0:2])
+            else:
+                nc.vector.tensor_copy(out=dst[:, :32], in_=src[:, :32, :, 0:2])
+                nc.scalar.copy(out=dst[:, 32:], in_=src[:, 32:, :, 0:2])
             nc.scalar.copy(out=w_bf[1][:, :, cols, :].rearrange("p t m j -> p m j t"), in_=src[:, :, :, 2:4])
             for t in range(2):
                 nc.vector.quantize_mx(
@@ -143,24 +145,23 @@ def tile_picked_ycin_deep_p_kernel(
         def take_a(t):
             nc.vector.tensor_tensor(ga[t][:], y[t][:].indirect(fa_sb[:]), m1_sb[:], MULT)
 
-        def take_b(t):
-            nc.vector.tensor_tensor(p1[t][:], y[t][:].indirect(fb_sb[:]), ga[t][:], MULT)
+        def take_b(t, lo, hi):
+            nc.vector.tensor_tensor(
+                p1[t][:, lo:hi], y[t][:].indirect(fb_sb[:, lo // 16 : hi // 16]), ga[t][:, lo:hi], MULT
+            )
 
-        def pair(t):
-            pv = p1[t][:].rearrange("p (h v d) -> p h d v", h=2, d=2)
-            turned_ps = psum.tile([P, 2, P], F32, name="turned_ps", bufs=2)
-            for h in range(2):
-                for d in range(2):
-                    nc.tensor.matmul(
-                        turned_ps[:, h, :], lhsT=pv[:, h, d, :], rhs=ident[:],
-                        start=(d == 0), stop=(d == 1), is_transpose=True,
-                    )
-            turned = sb.tile([P, 2, P], F32, name="turned", bufs=2)
+        def pair(t, h):
+            pv = p1[t][:, 2 * h * P : 2 * (h + 1) * P].rearrange("p (v d) -> p d v", d=2)
+            turned_ps = psum.tile([P, P], F32, name="turned_ps", bufs=2)
+            for d in range(2):
+                nc.tensor.matmul(
+                    turned_ps[:], lhsT=pv[:, d, :], rhs=ident[:], start=(d == 0), stop=(d == 1), is_transpose=True
+                )
+            turned = sb.tile([P, P], F32, name="turned", bufs=2)
             nc.scalar.copy(out=turned[:], in_=turned_ps[:])
-            back_ps = psum.tile([P, 2, P], F32, name="back_ps", bufs=2)
-            for h in range(2):
-                nc.tensor.transpose(back_ps[:, h, :], turned[:, h, :], ident[:])
-            nc.scalar.copy(out=x1[t][:], in_=back_ps[:].rearrange("p h v -> p (h v)"))
+            back_ps = psum.tile([P, P], F32, name="back_ps", bufs=2)
+            nc.tensor.transpose(back_ps[:], turned[:], ident[:])
+            nc.scalar.copy(out=x1[t][:, h * P : (h + 1) * P], in_=back_ps[:])
 
         def take_d(t):
             nc.vector.tensor_tensor(gd[t][:], y[t][:].indirect(fd_sb[:]), um[t][:], MULT)
@@ -173,10 +174,15 @@ def tile_picked_ycin_deep_p_kernel(
         for t in (0, 2):
             take_a(t)
             take_a(t + 1)
-            take_b(t)
-            pair(t)
-            take_b(t + 1)
-            pair(t + 1)
+            for u in (t, t + 1):
+                if u < PACK - 1:
+                    take_b(u, 0, S)
+                    pair(u, 0)
+                else:
+                    take_b(u, 0, S // 2)
+                    pair(u, 0)
+                    take_b(u, S // 2, S)
+                pair(u, 1)
         for t in range(PACK):
             take_d(t)
 
@@ -184,10 +190,10 @@ def tile_picked_ycin_deep_p_kernel(
         z_codes = [sb.tile([P, P], U32, name="z_codes%d" % h, align_bytes=64) for h in range(2)]
         z_scales = [sb.tile([P, P], U8, name="z_scales%d" % h, align_bytes=64) for h in range(2)]
 
-        def weave(h, copy):
+        def weave(h, lo, hi, copy):
             copy(
-                out=z_bf[h][:].rearrange("p (c i) t -> p c t i", i=4),
-                in_=z0[h][:].rearrange("p t (c i) -> p c t i", i=4),
+                out=z_bf[h][:, lo:hi, :].rearrange("p (c i) t -> p c t i", i=4),
+                in_=z0[h][:, :, lo:hi].rearrange("p t (c i) -> p c t i", i=4),
             )
 
         def quantize_z(h):
@@ -210,9 +216,10 @@ def tile_picked_ycin_deep_p_kernel(
 
         for t in range(PACK):
             take_c(t, 0)
-        weave(0, nc.scalar.copy)
+        weave(0, 0, P, nc.scalar.copy)
         for t in range(PACK):
             take_c(t, 1)
+        weave(1, P // 2, P, nc.scalar.copy)
         quantize_z(0)
         o_ps = psum.tile([P, 2, P], F32, name="mx_ps", bufs=4)
         for b in range(2):
@@ -221,7 +228,7 @@ def tile_picked_ycin_deep_p_kernel(
         nc.scalar.copy(out=o_first[:], in_=o_ps[:])
         nc.sync.dma_start(out=out[:, :P].rearrange("(b p) v -> p b v", p=P), in_=o_first[:])
 
-        weave(1, nc.vector.tensor_copy)
+        weave(1, 0, P // 2, nc.vector.tensor_copy)
         quantize_z(1)
         for b in range(2):
             o_ps = psum.tile([P, P], F32, name="mx_ps", bufs=4)

@@ -19,6 +19,7 @@ COPY = mybir.ActivationFunctionType.Copy
 P = 128
 PACK = 4
 SPARE = 8
+QUAD = P // PACK
 
 
 def tile_picked_ycin_deep_p_kernel(
@@ -38,163 +39,190 @@ def tile_picked_ycin_deep_p_kernel(
 
         xs_all = sb.tile([P, T], U8, name="xs_all", align_bytes=64)
         xw_all = sb.tile([P, T], U32, name="xw_all", align_bytes=64)
-        nc.gpsimd.memset(xs_all[:].bitcast(I32), 0)
+        nc.vector.memset(xs_all[:].bitcast(I32), 0)
+        w1_rows = w1.rearrange("(p j) c -> p j c", j=PACK)
+        w_raw0 = sb.tile([P, PACK, P], F32, name="w_raw0")
+        w_raw1 = sb.tile([P, PACK, P], F32, name="w_raw1")
+        w_raw23 = sb.tile([P, PACK, 2 * P], F32, name="w_raw23", tag="w_raw23", align_bytes=64)
+        m1_sb = sb.tile([P, S], F32, name="m1_sb")
+        m2_sb = [sb.tile([P, P], F32, name="m2_%d" % h, tag="m2_%d" % h, align_bytes=64) for h in range(2)]
+        unit_sb = sb.tile([P, PACK], F32, name="unit_sb")
+        t_raw = sb.tile([P, PACK, N], F32, name="t_raw")
+        nc.sync.dma_start(out=w_raw0[:], in_=w1_rows[:, :, :P])
+        nc.sync.dma_start(out=offs_sb[:], in_=offs)
+        for q in range(4):
+            (nc.sync if q >= 2 else nc.scalar).dma_start(
+                out=xs_all[32 * q : 32 * q + 4, :].bitcast(I32),
+                in_=x_scales[0, 4 * q : 4 * q + 4, :].bitcast(I32),
+            )
         nc.sync.dma_start(
             out=xw_all[:].bitcast(I32),
             in_=x_words[0].rearrange("p n t -> p (n t)").bitcast(I32),
         )
-        nc.sync.dma_start(out=offs_sb[:], in_=offs)
-        w1_rows = w1.rearrange("(p j) c -> p j c", j=PACK)
-        w_raw = [sb.tile([P, PACK, H // 2], F32, name="w_raw%d" % h) for h in range(2)]
-        nc.sync.dma_start(out=w_raw[0][:], in_=w1_rows[:, :, : H // 2])
-        for q in range(4):
-            nc.sync.dma_start(
-                out=xs_all[32 * q : 32 * q + 4, :].bitcast(I32),
-                in_=x_scales[0, 4 * q : 4 * q + 4, :].bitcast(I32),
-            )
-        nc.sync.dma_start(out=w_raw[1][:], in_=w1_rows[:, :, H // 2 :])
-        m1_sb = sb.tile([P, S], F32, name="m1_sb")
-        m2_sb = sb.tile([P, V], F32, name="m2_sb")
-        unit_sb = sb.tile([P, PACK], F32, name="unit_sb")
-        t_raw = sb.tile([P, PACK, N], F32, name="t_raw")
-        nc.sync.dma_start(out=t_raw[:], in_=t1.rearrange("(p j) n -> p j n", j=PACK))
+        nc.sync.dma_start(out=w_raw1[:], in_=w1_rows[:, :, P : 2 * P])
         nc.sync.dma_start(out=fa_sb[:], in_=fa)
         nc.sync.dma_start(out=m1_sb[:], in_=m1)
+        nc.sync.dma_start(out=w_raw23[:], in_=w1_rows[:, :, 2 * P :])
         nc.sync.dma_start(out=fb_sb[:], in_=fb)
-        nc.sync.dma_start(out=m2_sb[:], in_=m2)
+        nc.sync.dma_start(out=t_raw[:], in_=t1.rearrange("(p j) n -> p j n", j=PACK))
+        for h in range(2):
+            nc.sync.dma_start(out=m2_sb[h][:], in_=m2[:, h * P : (h + 1) * P])
         nc.sync.dma_start(out=unit_sb[:], in_=unit.rearrange("(p t) o -> p (t o)", t=PACK))
         nc.sync.dma_start(out=fd_sb[:], in_=fd)
         nc.sync.dma_start(out=fc_sb[:], in_=fc)
 
-        y = [sb.tile([P, S + SPARE], F32, name="y%d" % t) for t in range(PACK)]
+        y = [sb.tile([P, S + SPARE], F32, name="y%d" % u) for u in range(PACK)]
+        y_dealt = [sb.tile([P, S], F32, name="y_dealt%d" % t, tag="y_dealt%d" % t, align_bytes=64) for t in range(PACK)]
         x1 = [sb.tile([P, V], F32, name="x1_%d" % t) for t in range(PACK)]
-        for t in range(PACK):
-            nc.vector.memset(y[t][:, S:], 0.0)
+        for u in range(PACK):
+            nc.vector.memset(y[u][:, S:], 0.0)
 
         ident = sb.tile([P, P], F32, name="ident")
         make_identity(nc, ident[:])
 
-        xs = sb.tile([P, S], U8, name="xs", align_bytes=64)
+        def bank(shape):
+            return psum.tile(shape, F32, name="bank", bufs=8)
+
+        def interleave(dst, src, copy):
+            copy(
+                out=dst.rearrange("p (c i) j -> p c j i", i=4),
+                in_=src.rearrange("p j (c i) -> p c j i", i=4),
+            )
+
+        def cast(raw, name, copy, tag=None):
+            bf = sb.tile([P, raw.shape[2], PACK], BF16, name=name, tag=tag or name, align_bytes=64)
+            interleave(bf[:], raw, copy)
+            return bf
+
+        def quantize(bf, name, codes_tag=None):
+            width = bf.shape[1]
+            codes = sb.tile([P, width], U32, name=name + "_codes", tag=codes_tag or name + "_codes", align_bytes=64)
+            scales = sb.tile([P, width], U8, name=name + "_scales", align_bytes=64)
+            nc.vector.quantize_mx(
+                out=codes[:].bitcast(FP8X4), scales=scales[:], in_=bf[:].rearrange("p n j -> p (n j)")
+            )
+            return codes, scales
+
+        HALF = S // 2
         xw = sb.tile([P, S], U32, name="xw", align_bytes=64)
-        nc.vector.tensor_copy(out=xw[:], in_=xw_all[:].indirect(offs_sb[:]))
-        nc.vector.tensor_copy(out=xs[:], in_=xs_all[:].indirect(offs_sb[:]))
+        xs = sb.tile([P, S], U8, name="xs", align_bytes=64)
 
-        w_bf = [sb.tile([P, 2, P, PACK], BF16, name="w_bf%d" % u, align_bytes=64) for u in range(2)]
-        w_codes = [sb.tile([P, 2, P], U32, name="w_codes%d" % u, align_bytes=64) for u in range(2)]
-        w_scales = [sb.tile([P, 2, P], U8, name="w_scales%d" % u, align_bytes=64) for u in range(2)]
-        for h in range(2):
-            src = w_raw[h][:].rearrange("p j (m t) -> p m j t", t=PACK)
-            cols = slice(h * (P // 2), (h + 1) * (P // 2))
-            dst = w_bf[0][:, :, cols, :].rearrange("p t m j -> p m j t")
-            if h == 0:
-                nc.scalar.copy(out=dst, in_=src[:, :, :, 0:2])
-            else:
-                nc.vector.tensor_copy(out=dst[:, :32], in_=src[:, :32, :, 0:2])
-                nc.scalar.copy(out=dst[:, 32:], in_=src[:, 32:, :, 0:2])
-            nc.scalar.copy(out=w_bf[1][:, :, cols, :].rearrange("p t m j -> p m j t"), in_=src[:, :, :, 2:4])
-            for t in range(2):
-                nc.vector.quantize_mx(
-                    out=w_codes[0][:, t, cols].bitcast(FP8X4),
-                    scales=w_scales[0][:, t, cols],
-                    in_=w_bf[0][:, t, cols, :].rearrange("p m j -> p (m j)"),
-                )
+        def pick(dst, window, lo, hi):
+            nc.vector.tensor_copy(out=dst, in_=window[:].indirect(offs_sb[:, lo // 16 : hi // 16]))
 
-        def project(t, cols, copy):
-            y_ps = psum.tile([P, cols.stop - cols.start], F32, name="mx_ps", bufs=4)
+        def multiply(dst, packed, first, lo, hi):
             nc.tensor.matmul_mx(
-                out=y_ps[:],
-                lhsT=w_codes[t // 2][:, t % 2, :].bitcast(FP8X4),
-                lhsT_scale=w_scales[t // 2][:, t % 2, :],
-                rhs=xw[:, cols].bitcast(FP8X4),
-                rhs_scale=xs[:, cols],
+                out=dst,
+                lhsT=packed[0][:, first : first + P].bitcast(FP8X4),
+                lhsT_scale=packed[1][:, first : first + P],
+                rhs=xw[:, lo:hi].bitcast(FP8X4),
+                rhs_scale=xs[:, lo:hi],
                 start=True,
                 stop=True,
             )
-            copy(out=y[t][:, cols], in_=y_ps[:])
 
-        project(0, slice(0, S // 2), nc.scalar.copy)
-        project(0, slice(S // 2, S), nc.scalar.copy)
-        project(1, slice(0, S), nc.scalar.copy)
-        nc.vector.quantize_mx(
-            out=w_codes[1][:].rearrange("p t m -> p (t m)").bitcast(FP8X4),
-            scales=w_scales[1][:].rearrange("p t m -> p (t m)"),
-            in_=w_bf[1][:].rearrange("p t m j -> p (t m j)"),
-        )
-        project(2, slice(0, S), nc.scalar.copy)
-        project(3, slice(0, S), nc.scalar.copy)
+        def project_part(u, packed, first, lo, hi):
+            y_ps = bank([P, hi - lo])
+            multiply(y_ps[:], packed, first, lo, hi)
+            nc.scalar.copy(out=y[u][:, lo:hi], in_=y_ps[:])
 
-        t_bf = sb.tile([P, N, PACK], BF16, name="t_bf", align_bytes=64)
-        nc.vector.tensor_copy(
-            out=t_bf[:].rearrange("p (c i) j -> p c j i", i=4),
-            in_=t_raw[:].rearrange("p j (c i) -> p c j i", i=4),
-        )
-        t_codes = sb.tile([P, N], U32, name="t_codes", align_bytes=64)
-        t_scales = sb.tile([P, N], U8, name="t_scales", align_bytes=64)
-        nc.vector.quantize_mx(
-            out=t_codes[:].bitcast(FP8X4), scales=t_scales[:], in_=t_bf[:].rearrange("p n j -> p (n j)")
-        )
-        um = [sb.tile([P, V], F32, name="um%d" % t) for t in range(PACK)]
-        for t in range(PACK):
-            nc.scalar.activation(out=um[t][:], in_=m2_sb[:], func=COPY, scale=unit_sb[:, t : t + 1])
+        def project(u, packed, first):
+            y_ps = bank([P, S])
+            multiply(y_ps[:], packed, first, 0, S)
+            nc.scalar.copy(out=y[u][:, :S], in_=y_ps[:])
 
-        ga = [sb.tile([P, S], F32, name="ga%d" % t) for t in range(PACK)]
-        p1 = [sb.tile([P, S], F32, name="p1_%d" % t) for t in range(PACK)]
-        gd = [sb.tile([P, V], F32, name="gd%d" % t) for t in range(PACK)]
-        z0 = [sb.tile([P, PACK, P], F32, name="z0_%d" % h) for h in range(2)]
+        def deal(u):
+            for t in range(PACK):
+                nc.sync.dma_start(out=y_dealt[t][QUAD * u : QUAD * (u + 1), :], in_=y[u][t:P:PACK, :S])
 
-        def take_a(t):
-            nc.vector.tensor_tensor(ga[t][:], y[t][:].indirect(fa_sb[:]), m1_sb[:], MULT)
+        pick(xs[:], xs_all, 0, S)
+        w_packed0 = quantize(cast(w_raw0[:], "w0_bf", nc.scalar.copy), "w0")
+        for lo, hi in ((0, HALF), (HALF, HALF + P), (HALF + P, S)):
+            pick(xw[:, lo:hi], xw_all, lo, hi)
+            project_part(0, w_packed0, 0, lo, hi)
+        deal(0)
+        w_packed1 = quantize(cast(w_raw1[:], "w1_bf", nc.scalar.copy), "w1")
+        project(1, w_packed1, 0)
+        deal(1)
 
-        def take_b(t, lo, hi):
+        ga = [sb.tile([P, S], F32, name="ga%d" % u) for u in range(PACK)]
+        turned = [sb.tile([P, PACK, P], F32, name="turned%d" % h) for h in range(2)]
+
+        def take_a(u):
+            nc.vector.tensor_tensor(ga[u][:], y[u][:].indirect(fa_sb[:]), m1_sb[:], MULT)
+
+        def take_b(u, lo, hi):
             nc.vector.tensor_tensor(
-                p1[t][:, lo:hi], y[t][:].indirect(fb_sb[:, lo // 16 : hi // 16]), ga[t][:, lo:hi], MULT
+                p1[u][:, lo:hi], y[u][:].indirect(fb_sb[:, lo // 16 : hi // 16]), ga[u][:, lo:hi], MULT
             )
 
-        def pair(t, h):
-            pv = p1[t][:, 2 * h * P : 2 * (h + 1) * P].rearrange("p (v d) -> p d v", d=2)
-            turned_ps = psum.tile([P, P], F32, name="turned_ps", bufs=2)
+        def pair(u, h):
+            pv = p1[u][:, 2 * h * P : 2 * (h + 1) * P].rearrange("p (v d) -> p d v", d=2)
+            turned_ps = bank([P, P])
             for d in range(2):
                 nc.tensor.matmul(
                     turned_ps[:], lhsT=pv[:, d, :], rhs=ident[:], start=(d == 0), stop=(d == 1), is_transpose=True
                 )
-            turned = sb.tile([P, P], F32, name="turned", bufs=2)
-            nc.scalar.copy(out=turned[:], in_=turned_ps[:])
-            back_ps = psum.tile([P, P], F32, name="back_ps", bufs=2)
-            nc.tensor.transpose(back_ps[:], turned[:], ident[:])
-            nc.scalar.copy(out=x1[t][:, h * P : (h + 1) * P], in_=back_ps[:])
+            nc.scalar.copy(
+                out=turned[h][:, :, QUAD * u : QUAD * (u + 1)],
+                in_=turned_ps[:].rearrange("v (m t) -> v t m", t=PACK),
+            )
 
-        def take_d(t):
-            nc.vector.tensor_tensor(gd[t][:], y[t][:].indirect(fd_sb[:]), um[t][:], MULT)
+        take_a(0)
+        take_a(1)
+        w_packed23 = quantize(cast(w_raw23[:], "w23_bf", nc.scalar.copy, "w1_codes"), "w23")
+        for u in (2, 3):
+            project(u, w_packed23, (u - 2) * P)
+            deal(u)
+        p1 = [
+            sb.tile([P, S], F32, name="p1_%d" % u, tag=("w1_codes", "w_raw23", "p1_2", "p1_3")[u], align_bytes=64)
+            for u in range(PACK)
+        ]
+        for u in (0, 1):
+            take_b(u, 0, S)
+            pair(u, 0)
+            pair(u, 1)
+        take_a(2)
+        take_a(3)
+        t_bf = cast(t_raw[:], "t_bf", nc.scalar.copy)
+        take_b(2, 0, S)
+        pair(2, 0)
+        pair(2, 1)
+        take_b(3, 0, S // 2)
+        pair(3, 0)
+        take_b(3, S // 2, S)
+        pair(3, 1)
+        for t in range(PACK):
+            back_ps = bank([P, 2, P])
+            for h in range(2):
+                nc.tensor.transpose(back_ps[:, h, :], turned[h][:, t, :], ident[:])
+            nc.scalar.activation(
+                out=x1[t][:], in_=back_ps[:].rearrange("p h v -> p (h v)"), func=COPY, scale=unit_sb[:, t : t + 1]
+            )
+
+        gd = [sb.tile([P, V], F32, name="gd%d" % t) for t in range(PACK)]
+        for t in range(PACK):
+            for h in range(2):
+                nc.vector.tensor_tensor(
+                    gd[t][:, h * P : (h + 1) * P], y_dealt[t][:].indirect(fd_sb[:, 8 * h : 8 * h + 8]), m2_sb[h][:], MULT
+                )
+
+        t_codes, t_scales = quantize(t_bf, "t", "m2_0")
+        z0 = [
+            sb.tile([P, PACK, P], F32, name="z0_%d" % h, tag=("y_dealt3", "m2_1")[h], align_bytes=64) for h in range(2)
+        ]
 
         def take_c(t, h):
             nc.vector.tensor_tensor(
                 z0[h][:, t, :], x1[t][:].indirect(fc_sb[:, 8 * h : 8 * h + 8]), gd[t][:, h * P : (h + 1) * P], MULT
             )
 
-        for t in (0, 2):
-            take_a(t)
-            take_a(t + 1)
-            for u in (t, t + 1):
-                if u < PACK - 1:
-                    take_b(u, 0, S)
-                    pair(u, 0)
-                else:
-                    take_b(u, 0, S // 2)
-                    pair(u, 0)
-                    take_b(u, S // 2, S)
-                pair(u, 1)
-        for t in range(PACK):
-            take_d(t)
-
         z_bf = [sb.tile([P, P, PACK], BF16, name="z_bf%d" % h, align_bytes=64) for h in range(2)]
         z_codes = [sb.tile([P, P], U32, name="z_codes%d" % h, align_bytes=64) for h in range(2)]
         z_scales = [sb.tile([P, P], U8, name="z_scales%d" % h, align_bytes=64) for h in range(2)]
 
         def weave(h, lo, hi, copy):
-            copy(
-                out=z_bf[h][:, lo:hi, :].rearrange("p (c i) t -> p c t i", i=4),
-                in_=z0[h][:, :, lo:hi].rearrange("p t (c i) -> p c t i", i=4),
-            )
+            interleave(z_bf[h][:, lo:hi, :], z0[h][:, :, lo:hi], copy)
 
         def quantize_z(h):
             nc.vector.quantize_mx(
@@ -221,7 +249,7 @@ def tile_picked_ycin_deep_p_kernel(
             take_c(t, 1)
         weave(1, P // 2, P, nc.scalar.copy)
         quantize_z(0)
-        o_ps = psum.tile([P, 2, P], F32, name="mx_ps", bufs=4)
+        o_ps = bank([P, 2, P])
         for b in range(2):
             product(0, b, o_ps[:, b, :])
         o_first = sb.tile([P, 2, P], F32, name="o_first")
@@ -231,7 +259,7 @@ def tile_picked_ycin_deep_p_kernel(
         weave(1, 0, P // 2, nc.vector.tensor_copy)
         quantize_z(1)
         for b in range(2):
-            o_ps = psum.tile([P, P], F32, name="mx_ps", bufs=4)
+            o_ps = bank([P, P])
             product(1, b, o_ps[:])
             o_sb = sb.tile([P, P], F32, name="o_sb%d" % b)
             if b == 0:

from contextlib import ExitStack

import concourse.mybir as mybir
from concourse.masks import make_identity

K, T, S, H, N, V = 512, 1024, 512, 512, 256, 256
FLOPS = 2 * K * H * S + 2 * H * N * V

F32 = mybir.dt.float32
BF16 = mybir.dt.bfloat16
I32 = mybir.dt.int32
U32 = mybir.dt.uint32
U16 = mybir.dt.uint16
U8 = mybir.dt.uint8
FP8X4 = mybir.dt.float8_e4m3fn_x4
MULT = mybir.AluOpType.mult
COPY = mybir.ActivationFunctionType.Copy

P = 128
PACK = 4
SPARE = 8
QUAD = P // PACK


def tile_picked_ycin_deep_p_kernel(
    tc, x_words, x_scales, w1, m1, m2, unit, t1, offs, fa, fb, fc, fd, out
):
    nc = tc.nc
    with ExitStack() as ctx:
        lists = ctx.enter_context(tc.tile_pool(name="lists", bufs=1))
        sb = ctx.enter_context(tc.tile_pool(name="sb", bufs=1))
        psum = ctx.enter_context(tc.psum_pool(name="psum", bufs=1))

        offs_sb = lists.tile([P, S // 16], U16, name="offs_sb")
        fa_sb = lists.tile([P, S // 16], U16, name="fa_sb")
        fb_sb = lists.tile([P, S // 16], U16, name="fb_sb")
        fc_sb = lists.tile([P, V // 16], U16, name="fc_sb")
        fd_sb = lists.tile([P, V // 16], U16, name="fd_sb")

        xs_all = sb.tile([P, T], U8, name="xs_all", align_bytes=64)
        xw_all = sb.tile([P, T], U32, name="xw_all", align_bytes=64)
        nc.vector.memset(xs_all[:].bitcast(I32), 0)
        w1_rows = w1.rearrange("(p j) c -> p j c", j=PACK)
        w_raw0 = sb.tile([P, PACK, P], F32, name="w_raw0")
        w_raw1 = sb.tile([P, PACK, P], F32, name="w_raw1")
        w_raw23 = sb.tile([P, PACK, 2 * P], F32, name="w_raw23", tag="w_raw23", align_bytes=64)
        m1_sb = sb.tile([P, S], F32, name="m1_sb")
        m2_sb = [sb.tile([P, P], F32, name="m2_%d" % h, tag="m2_%d" % h, align_bytes=64) for h in range(2)]
        unit_sb = sb.tile([P, PACK], F32, name="unit_sb")
        t_raw = sb.tile([P, PACK, N], F32, name="t_raw")
        nc.sync.dma_start(out=w_raw0[:], in_=w1_rows[:, :, :P])
        nc.sync.dma_start(out=offs_sb[:], in_=offs)
        for q in range(4):
            (nc.sync if q >= 2 else nc.scalar).dma_start(
                out=xs_all[32 * q : 32 * q + 4, :].bitcast(I32),
                in_=x_scales[0, 4 * q : 4 * q + 4, :].bitcast(I32),
            )
        nc.sync.dma_start(
            out=xw_all[:].bitcast(I32),
            in_=x_words[0].rearrange("p n t -> p (n t)").bitcast(I32),
        )
        nc.sync.dma_start(out=w_raw1[:], in_=w1_rows[:, :, P : 2 * P])
        nc.sync.dma_start(out=fa_sb[:], in_=fa)
        nc.sync.dma_start(out=m1_sb[:], in_=m1)
        nc.sync.dma_start(out=w_raw23[:], in_=w1_rows[:, :, 2 * P :])
        nc.sync.dma_start(out=fb_sb[:], in_=fb)
        nc.sync.dma_start(out=t_raw[:], in_=t1.rearrange("(p j) n -> p j n", j=PACK))
        for h in range(2):
            nc.sync.dma_start(out=m2_sb[h][:], in_=m2[:, h * P : (h + 1) * P])
        nc.sync.dma_start(out=unit_sb[:], in_=unit.rearrange("(p t) o -> p (t o)", t=PACK))
        nc.sync.dma_start(out=fd_sb[:], in_=fd)
        nc.sync.dma_start(out=fc_sb[:], in_=fc)

        y = [sb.tile([P, S + SPARE], F32, name="y%d" % u) for u in range(PACK)]
        y_dealt = [sb.tile([P, S], F32, name="y_dealt%d" % t, tag="y_dealt%d" % t, align_bytes=64) for t in range(PACK)]
        x1 = [sb.tile([P, V], F32, name="x1_%d" % t) for t in range(PACK)]
        for u in range(PACK):
            nc.vector.memset(y[u][:, S:], 0.0)

        ident = sb.tile([P, P], F32, name="ident")
        make_identity(nc, ident[:])

        def bank(shape):
            return psum.tile(shape, F32, name="bank", bufs=8)

        def interleave(dst, src, copy):
            copy(
                out=dst.rearrange("p (c i) j -> p c j i", i=4),
                in_=src.rearrange("p j (c i) -> p c j i", i=4),
            )

        def cast(raw, name, copy, tag=None):
            bf = sb.tile([P, raw.shape[2], PACK], BF16, name=name, tag=tag or name, align_bytes=64)
            interleave(bf[:], raw, copy)
            return bf

        def quantize(bf, name, codes_tag=None):
            width = bf.shape[1]
            codes = sb.tile([P, width], U32, name=name + "_codes", tag=codes_tag or name + "_codes", align_bytes=64)
            scales = sb.tile([P, width], U8, name=name + "_scales", align_bytes=64)
            nc.vector.quantize_mx(
                out=codes[:].bitcast(FP8X4), scales=scales[:], in_=bf[:].rearrange("p n j -> p (n j)")
            )
            return codes, scales

        HALF = S // 2
        xw = sb.tile([P, S], U32, name="xw", align_bytes=64)
        xs = sb.tile([P, S], U8, name="xs", align_bytes=64)

        def pick(dst, window, lo, hi):
            nc.vector.tensor_copy(out=dst, in_=window[:].indirect(offs_sb[:, lo // 16 : hi // 16]))

        def multiply(dst, packed, first, lo, hi):
            nc.tensor.matmul_mx(
                out=dst,
                lhsT=packed[0][:, first : first + P].bitcast(FP8X4),
                lhsT_scale=packed[1][:, first : first + P],
                rhs=xw[:, lo:hi].bitcast(FP8X4),
                rhs_scale=xs[:, lo:hi],
                start=True,
                stop=True,
            )

        def project_part(u, packed, first, lo, hi):
            y_ps = bank([P, hi - lo])
            multiply(y_ps[:], packed, first, lo, hi)
            nc.scalar.copy(out=y[u][:, lo:hi], in_=y_ps[:])

        def project(u, packed, first):
            y_ps = bank([P, S])
            multiply(y_ps[:], packed, first, 0, S)
            nc.scalar.copy(out=y[u][:, :S], in_=y_ps[:])

        def deal(u):
            for t in range(PACK):
                nc.sync.dma_start(out=y_dealt[t][QUAD * u : QUAD * (u + 1), :], in_=y[u][t:P:PACK, :S])

        pick(xs[:], xs_all, 0, S)
        w_packed0 = quantize(cast(w_raw0[:], "w0_bf", nc.scalar.copy), "w0")
        for lo, hi in ((0, HALF), (HALF, HALF + P), (HALF + P, S)):
            pick(xw[:, lo:hi], xw_all, lo, hi)
            project_part(0, w_packed0, 0, lo, hi)
        deal(0)
        w_packed1 = quantize(cast(w_raw1[:], "w1_bf", nc.scalar.copy), "w1")
        project(1, w_packed1, 0)
        deal(1)

        ga = [sb.tile([P, S], F32, name="ga%d" % u) for u in range(PACK)]
        turned = [sb.tile([P, PACK, P], F32, name="turned%d" % h) for h in range(2)]

        def take_a(u):
            nc.vector.tensor_tensor(ga[u][:], y[u][:].indirect(fa_sb[:]), m1_sb[:], MULT)

        def take_b(u, lo, hi):
            nc.vector.tensor_tensor(
                p1[u][:, lo:hi], y[u][:].indirect(fb_sb[:, lo // 16 : hi // 16]), ga[u][:, lo:hi], MULT
            )

        def pair(u, h):
            pv = p1[u][:, 2 * h * P : 2 * (h + 1) * P].rearrange("p (v d) -> p d v", d=2)
            turned_ps = bank([P, P])
            for d in range(2):
                nc.tensor.matmul(
                    turned_ps[:], lhsT=pv[:, d, :], rhs=ident[:], start=(d == 0), stop=(d == 1), is_transpose=True
                )
            nc.scalar.copy(
                out=turned[h][:, :, QUAD * u : QUAD * (u + 1)],
                in_=turned_ps[:].rearrange("v (m t) -> v t m", t=PACK),
            )

        take_a(0)
        take_a(1)
        w_packed23 = quantize(cast(w_raw23[:], "w23_bf", nc.scalar.copy, "w1_codes"), "w23")
        for u in (2, 3):
            project(u, w_packed23, (u - 2) * P)
            deal(u)
        p1 = [
            sb.tile([P, S], F32, name="p1_%d" % u, tag=("w1_codes", "w_raw23", "p1_2", "p1_3")[u], align_bytes=64)
            for u in range(PACK)
        ]
        for u in (0, 1):
            take_b(u, 0, S)
            pair(u, 0)
            pair(u, 1)
        take_a(2)
        take_a(3)
        t_bf = cast(t_raw[:], "t_bf", nc.scalar.copy)
        take_b(2, 0, S)
        pair(2, 0)
        pair(2, 1)
        take_b(3, 0, S // 2)
        pair(3, 0)
        take_b(3, S // 2, S)
        pair(3, 1)
        for t in range(PACK):
            back_ps = bank([P, 2, P])
            for h in range(2):
                nc.tensor.transpose(back_ps[:, h, :], turned[h][:, t, :], ident[:])
            nc.scalar.activation(
                out=x1[t][:], in_=back_ps[:].rearrange("p h v -> p (h v)"), func=COPY, scale=unit_sb[:, t : t + 1]
            )

        gd = [sb.tile([P, V], F32, name="gd%d" % t) for t in range(PACK)]
        for t in range(PACK):
            for h in range(2):
                nc.vector.tensor_tensor(
                    gd[t][:, h * P : (h + 1) * P], y_dealt[t][:].indirect(fd_sb[:, 8 * h : 8 * h + 8]), m2_sb[h][:], MULT
                )

        t_codes, t_scales = quantize(t_bf, "t", "m2_0")
        z0 = [
            sb.tile([P, PACK, P], F32, name="z0_%d" % h, tag=("y_dealt3", "m2_1")[h], align_bytes=64) for h in range(2)
        ]

        def take_c(t, h):
            nc.vector.tensor_tensor(
                z0[h][:, t, :], x1[t][:].indirect(fc_sb[:, 8 * h : 8 * h + 8]), gd[t][:, h * P : (h + 1) * P], MULT
            )

        z_bf = [sb.tile([P, P, PACK], BF16, name="z_bf%d" % h, align_bytes=64) for h in range(2)]
        z_codes = [sb.tile([P, P], U32, name="z_codes%d" % h, align_bytes=64) for h in range(2)]
        z_scales = [sb.tile([P, P], U8, name="z_scales%d" % h, align_bytes=64) for h in range(2)]

        def weave(h, lo, hi, copy):
            interleave(z_bf[h][:, lo:hi, :], z0[h][:, :, lo:hi], copy)

        def quantize_z(h):
            nc.vector.quantize_mx(
                out=z_codes[h][:].bitcast(FP8X4),
                scales=z_scales[h][:],
                in_=z_bf[h][:].rearrange("p v t -> p (v t)"),
            )

        def product(h, b, dst):
            nc.tensor.matmul_mx(
                out=dst,
                lhsT=t_codes[:, b * P : (b + 1) * P].bitcast(FP8X4),
                lhsT_scale=t_scales[:, b * P : (b + 1) * P],
                rhs=z_codes[h][:].bitcast(FP8X4),
                rhs_scale=z_scales[h][:],
                start=True,
                stop=True,
            )

        for t in range(PACK):
            take_c(t, 0)
        weave(0, 0, P, nc.scalar.copy)
        for t in range(PACK):
            take_c(t, 1)
        weave(1, P // 2, P, nc.scalar.copy)
        quantize_z(0)
        o_ps = bank([P, 2, P])
        for b in range(2):
            product(0, b, o_ps[:, b, :])
        o_first = sb.tile([P, 2, P], F32, name="o_first")
        nc.scalar.copy(out=o_first[:], in_=o_ps[:])
        nc.sync.dma_start(out=out[:, :P].rearrange("(b p) v -> p b v", p=P), in_=o_first[:])

        weave(1, 0, P // 2, nc.vector.tensor_copy)
        quantize_z(1)
        for b in range(2):
            o_ps = bank([P, P])
            product(1, b, o_ps[:])
            o_sb = sb.tile([P, P], F32, name="o_sb%d" % b)
            if b == 0:
                nc.vector.tensor_copy(out=o_sb[:], in_=o_ps[:])
                nc.sync.dma_start(out=out[b * P : (b + 1) * P, P:], in_=o_sb[:])
            else:
                nc.scalar.copy(out=o_sb[:], in_=o_ps[:])
                nc.scalar.dma_start(out=out[b * P : (b + 1) * P, P:], in_=o_sb[:])
